import numpy as np
import ml_dtypes


def mxq(x, axis, fmt="e4m3"):
    dtype, down = {"e4m3": (ml_dtypes.float8_e4m3fn, 7), "e5m2": (ml_dtypes.float8_e5m2, 14)}[fmt]
    v = np.moveaxis(np.asarray(x, np.float32).astype(ml_dtypes.bfloat16).astype(np.float64), axis, -1)
    blocks = v.reshape(v.shape[:-1] + (-1, 32))
    amax = np.abs(blocks).max(-1, keepdims=True)
    byte = np.maximum(np.where(amax > 0, np.frexp(amax)[1] - 1 + 127, 0) - down, 1)
    scale = np.exp2(byte - 127.0)
    codes = (blocks / scale).astype(np.float32).astype(dtype).astype(np.float64)
    return np.moveaxis((codes * scale).reshape(v.shape), -1, axis)


WIDE = False


def mx_kscale(k):
    if not WIDE:
        return np.ones(k)
    levels = np.array([30, -30])
    if k % 512:
        return np.exp2(np.random.permutation(np.resize(levels, k // 32))).repeat(32)
    a = np.empty((k // 512, 16))
    for p in range(k // 512):
        a[p, :8] = np.random.permutation(np.resize(levels, 8))
        for g in range(8):
            far = levels[np.abs(levels - a[p, g]) >= 10]
            a[p, g + 8] = far[np.random.randint(len(far))]
    return np.exp2(a.ravel()).repeat(32)


def f64(x):
    return np.asarray(x).astype(np.float64)


def striped(idx):
    return np.tile(np.asarray(idx).reshape(-1, 16).T, (8, 1)).astype(np.uint16)


def unstriped(offs):
    return offs[:16].T.reshape(-1).astype(np.int64)


E2M1 = np.array([0.0, 0.5, 1.0, 1.5, 2.0, 3.0, 4.0, 6.0, -0.0, -0.5, -1.0, -1.5, -2.0, -3.0, -4.0, -6.0])


def pack_weight(w, fmt):
    k, n = w.shape
    w = f64(np.asarray(w, np.float32).astype(ml_dtypes.bfloat16)).reshape(k // 32, 32, n)
    amax = np.abs(w).max(1)
    if fmt == "e4m3":
        byte = np.frexp(amax)[1] - 1 + 127 - 7
    else:
        mant, ex = np.frexp(amax / 6.0)
        byte = np.where(mant > 0.5, ex, ex - 1) + 127
    byte = np.clip(np.where(amax > 0, byte, 1), 1, 254)
    scaled = (w * np.exp2(127.0 - byte)[:, None, :]).reshape(k, n).astype(np.float32)
    by_word = np.ascontiguousarray(scaled.reshape(k // 512, 128, 4, n).transpose(0, 1, 3, 2))
    if fmt == "e4m3":
        words = by_word.astype(ml_dtypes.float8_e4m3fn).view(np.uint8)
    else:
        c = by_word.astype(ml_dtypes.float4_e2m1fn).view(np.uint8) & 0xF
        words = (c[..., 0::2] | (c[..., 1::2] << 4)).reshape(k // 512, 128, 2 * n)
    return np.ascontiguousarray(words), np.ascontiguousarray(byte.astype(np.uint8).reshape(k // 512, 16, n))


def unpack_weight(words, scales, fmt):
    g, _, n = scales.shape
    words = np.ascontiguousarray(words).reshape(g, 128, n, -1)
    if fmt == "e4m3":
        vals = words.view(ml_dtypes.float8_e4m3fn).astype(np.float64)
    else:
        nib = np.empty((g, 128, n, 4), np.uint8)
        nib[..., 0::2] = words & 0xF
        nib[..., 1::2] = words >> 4
        vals = E2M1[nib]
    vals = vals * np.repeat(np.exp2(scales.astype(np.float64) - 127.0), 8, axis=1)[..., None]
    return vals.transpose(0, 1, 3, 2).reshape(g * 512, n)


def sigmoid(v):
    return 1.0 / (1.0 + np.exp(-v))


K, T, J, R, F, Z, N, M = 512, 512, 256, 512, 512, 1024, 256, 512


def setup_inputs():
    n = np.random.standard_normal
    idx = np.random.permutation(T)[:J]
    idx2 = np.random.permutation(Z)[:J]
    idx3 = np.random.permutation(M)[:J]
    fk = mx_kscale(K)
    fr = mx_kscale(R)
    ff = mx_kscale(F)
    xtp = pack_weight(n((K, T)) / fk[:, None], "e4m3")
    wp = pack_weight(n((K, R)) * 1 / np.sqrt(K) * fk[:, None] * fr, "e2m1")
    w2p = pack_weight(n((F, R)) * 1 / np.sqrt(F) * ff[:, None] * fr, "e2m1")
    wbp = pack_weight(n((R, N)) * 1 / np.sqrt(R) / fr[:, None], "e2m1")
    return {
        "xt_words": xtp[0],
        "xt_scales": xtp[1],
        "w_words": wp[0],
        "w_scales": wp[1],
        "xo": (n((F, Z))).astype(np.float32),
        "fl": (np.random.uniform(0.5, 2.0, (F, 1)) / ff[:, None]).astype(np.float32),
        "so": (n((F, J))).astype(np.float32),
        "w2_words": w2p[0],
        "w2_scales": w2p[1],
        "wb_words": wbp[0],
        "wb_scales": wbp[1],
        "tz": (n((N, M)) * 0.6).astype(np.float32),
        "rw": (np.random.uniform(0.5, 2.0, (1, J))).astype(np.float32),
        "offs": striped(idx),
        "offs2": striped(idx2),
        "offs3": striped(idx3),
    }


def reference(xt_words, xt_scales, w_words, w_scales, xo, fl, so, w2_words, w2_scales, wb_words, wb_scales, tz, rw, offs, offs2, offs3):
    idx = unstriped(offs)
    idx2 = unstriped(offs2)
    idx3 = unstriped(offs3)
    xtu = unpack_weight(xt_words, xt_scales, "e4m3")
    wu = unpack_weight(w_words, w_scales, "e2m1")
    w2u = unpack_weight(w2_words, w2_scales, "e2m1")
    wbu = unpack_weight(wb_words, wb_scales, "e2m1")
    u2 = f64(xo)[:, idx2] * sigmoid(f64(so)) * f64(fl)
    xtidxg = xtu[:, idx]
    a = wu.T @ xtidxg
    u2q = mxq(u2, 0, "e5m2")
    q = w2u.T @ u2q
    y1 = np.pad(q, ((0, 0), (1, 0)))[:, :J]
    hid = np.maximum(a, q - 0.6 * y1)
    hidq = mxq(hid, 0, "e5m2")
    p = wbu.T @ hidq
    y = np.maximum(p, f64(tz)[:, idx3]) * f64(rw)
    return y

@@ -1,0 +1,235 @@
+from contextlib import ExitStack
+
+import concourse.mybir as mybir
+from concourse.masks import make_identity
+
+K, T, J, R, F, Z, N, M = 512, 512, 256, 512, 512, 1024, 256, 512
+FLOPS = 2 * J * (K * R + F * R + R * N)
+
+F32 = mybir.dt.float32
+BF16 = mybir.dt.bfloat16
+I32 = mybir.dt.int32
+U32 = mybir.dt.uint32
+U16 = mybir.dt.uint16
+U8 = mybir.dt.uint8
+E4M3X4 = mybir.dt.float8_e4m3fn_x4
+E5M2X4 = mybir.dt.float8_e5m2_x4
+E2M1X4 = mybir.dt.float4_e2m1fn_x4
+ALU = mybir.AluOpType
+ACT = mybir.ActivationFunctionType
+
+P = 128
+PACK = 4
+HALVES = 2
+H = J // HALVES
+NT = N // P
+STEP = -0.6
+W_AT, W2_AT, WB_AT, XT_AT = 0, R, 2 * R, 2 * R + N
+PLANE_COLS = XT_AT + J
+
+
+def tile_list_two_picked_gated_stepgap_floored_kernel(
+    tc, xt_words, xt_scales, w_words, w_scales, xo, fl, so, w2_words, w2_scales,
+    wb_words, wb_scales, tz, rw, offs, offs2, offs3, out,
+):
+    nc = tc.nc
+    with ExitStack() as ctx:
+        sb = ctx.enter_context(tc.tile_pool(name="sb", bufs=1))
+        ps = ctx.enter_context(tc.psum_pool(name="ps", bufs=1))
+
+        def tile(name, shape, dtype):
+            return sb.tile(shape, dtype, name=name, align_bytes=64)
+
+        list_xt = tile("list_xt", [P, J // 16], U16)
+        list_xo = tile("list_xo", [P, J // 16], U16)
+        list_tz = tile("list_tz", [P, J // 16], U16)
+        so_sb = tile("so_sb", [P, PACK, J], F32)
+        xo_sb = [tile(f"xo_sb{t}", [P, Z], F32) for t in range(PACK)]
+        fl_sb = tile("fl_sb", [P, PACK], F32)
+        rw_sb = tile("rw_sb", [P, 2], F32)
+        tz_sb = tile("tz_sb", [P, NT, M], F32)
+        xt_raw = tile("xt_raw", [P, T], I32)
+        w_raw = tile("w_raw", [P, 2 * R], U8)
+        w2_raw = tile("w2_raw", [P, 2 * R], U8)
+        wb_sb = tile("wb_sb", [P, 2 * N], U8)
+        xs_raw = tile("xs_raw", [P, T], U8)
+        ws_raw = tile("ws_raw", [P, 2 * R], U8)
+        planes = tile("planes", [P, PLANE_COLS], U8)
+
+        nc.vector.memset(ws_raw[:].bitcast(I32), 0)
+        nc.vector.memset(xs_raw[:].bitcast(I32), 0)
+        nc.vector.memset(planes[:, WB_AT:XT_AT].bitcast(I32), 0)
+
+        xo_rows = xo.rearrange("(p t) z -> p t z", t=PACK)
+        nc.sync.dma_start(list_xo[:], offs2)
+        nc.sync.dma_start(so_sb[:], so.rearrange("(p t) j -> p t j", t=PACK))
+        nc.sync.dma_start(xo_sb[0][:], xo_rows[:, 0, :])
+        nc.sync.dma_start(list_xt[:], offs)
+        nc.scalar.dma_start(ws_raw[0:16, R : 2 * R].bitcast(I32), w2_scales[0].bitcast(I32))
+        nc.scalar.dma_start(ws_raw[0:16, 0:R].bitcast(I32), w_scales[0].bitcast(I32))
+        nc.scalar.dma_start(xs_raw[0:16, :].bitcast(I32), xt_scales[0].bitcast(I32))
+        nc.scalar.dma_start(planes[0:16, WB_AT:XT_AT].bitcast(I32), wb_scales[0].bitcast(I32))
+        nc.sync.dma_start(w2_raw[:].bitcast(I32), w2_words[0].bitcast(I32))
+        nc.sync.dma_start(list_tz[:], offs3)
+        for t in range(1, PACK):
+            nc.sync.dma_start(xo_sb[t][:], xo_rows[:, t, :])
+        nc.sync.dma_start(xt_raw[:], xt_words[0].rearrange("p c b -> p (c b)").bitcast(I32))
+        nc.sync.dma_start(w_raw[:].bitcast(I32), w_words[0].bitcast(I32))
+        nc.sync.dma_start(tz_sb[:], tz.rearrange("(u p) m -> p u m", p=P))
+        nc.gpsimd.dma_start(fl_sb[:], fl.rearrange("(p t) o -> p (t o)", t=PACK))
+        nc.gpsimd.dma_start(rw_sb[:], rw.rearrange("o (p e) -> p (o e)", e=2))
+        nc.gpsimd.dma_start(wb_sb[:].bitcast(I32), wb_words[0].bitcast(I32))
+
+        ident = tile("ident", [P, P], F32)
+        make_identity(nc, ident[:])
+        rw_ps = ps.tile([P, 2, P], F32, name="rw_ps")
+        for e in range(2):
+            nc.tensor.transpose(rw_ps[:, e, :], rw_sb[:, e : e + 1].to_broadcast([P, P]), ident[:])
+
+        sig = tile("sig", [P, PACK, J], F32)
+        gate = tile("gate", [P, PACK, J], F32)
+        for t in range(PACK):
+            nc.scalar.activation(sig[:, t, :], so_sb[:, t, :], ACT.Sigmoid)
+            nc.scalar.activation(gate[:, t, :], sig[:, t, :], ACT.Copy, scale=fl_sb[:, t : t + 1])
+
+        nc.vector.tensor_copy(
+            planes[:, W_AT:WB_AT].rearrange("p (s t m) -> p s t m", s=2, t=PACK),
+            ws_raw[:].rearrange("p (s m t) -> p s t m", s=2, t=PACK),
+        )
+        xs_picked = tile("xs_picked", [P, J], U8)
+        nc.vector.tensor_copy(xs_picked[:], xs_raw[:].indirect(list_xt[:]))
+        nc.vector.tensor_copy(planes[:, XT_AT:].bitcast(I32), xs_picked[:].bitcast(I32))
+        for quad in range(1, 4):
+            nc.scalar.dma_start(
+                planes[32 * quad : 32 * quad + 4, :].bitcast(I32),
+                planes[4 * quad : 4 * quad + 4, :].bitcast(I32),
+            )
+
+        def deal_words(dst, src):
+            nc.vector.tensor_copy(
+                dst[:].bitcast(U16).rearrange("p (t m) -> p t m", t=PACK),
+                src[:].bitcast(U16).rearrange("p (m t) -> p t m", t=PACK),
+            )
+
+        w2_sb = tile("w2_sb", [P, 2 * R], U8)
+        deal_words(w2_sb, w2_raw)
+
+        u2 = tile("u2", [P, PACK, J], F32)
+        for t in range(PACK - 1):
+            nc.vector.tensor_tensor(u2[:, t, :], xo_sb[t][:].indirect(list_xo[:]), gate[:, t, :], ALU.mult)
+        last = PACK - 1
+        for h in range(HALVES):
+            cols = slice(h * H, (h + 1) * H)
+            entries = list_xo[:, h * H // 16 : (h + 1) * H // 16]
+            nc.vector.tensor_tensor(u2[:, last, cols], xo_sb[last][:].indirect(entries), gate[:, last, cols], ALU.mult)
+
+        u2_bf = [tile(f"u2_bf{h}", [P, H * PACK], BF16) for h in range(HALVES)]
+        u2_codes = [tile(f"u2_codes{h}", [P, H], U32) for h in range(HALVES)]
+        u2_scales = [tile(f"u2_scales{h}", [P, H], U8) for h in range(HALVES)]
+        for h in range(HALVES):
+            nc.vector.tensor_copy(
+                u2_bf[h][:].rearrange("p (c i t) -> p c t i", i=4, t=PACK),
+                u2[:, :, h * H : (h + 1) * H].rearrange("p t (c i) -> p c t i", i=4),
+            )
+        for h in range(HALVES):
+            nc.vector.quantize_mx(u2_codes[h][:].bitcast(E5M2X4), u2_scales[h][:], u2_bf[h][:])
+
+        def first_stage(bank, words, plane_at, rhs, rhs_scale):
+            for t in range(PACK):
+                nc.tensor.matmul_mx(
+                    bank[:, t, :],
+                    lhsT=words[:, 2 * P * t : 2 * P * (t + 1)].bitcast(E2M1X4),
+                    lhsT_scale=planes[:, plane_at + P * t : plane_at + P * (t + 1)],
+                    rhs=rhs,
+                    rhs_scale=rhs_scale,
+                    start=True,
+                    stop=True,
+                )
+
+        q_ps = [ps.tile([P, PACK, H], F32, name=f"q_ps{h}") for h in range(HALVES)]
+        for h in range(HALVES):
+            first_stage(q_ps[h], w2_sb, W2_AT, u2_codes[h][:].bitcast(E5M2X4), u2_scales[h][:])
+
+        xt_picked = tile("xt_picked", [P, J], U32)
+        nc.vector.tensor_copy(xt_picked[:], xt_raw[:].bitcast(U32).indirect(list_xt[:]))
+        w_sb = tile("w_sb", [P, 2 * R], U8)
+        deal_words(w_sb, w_raw)
+        a_ps = [ps.tile([P, PACK, H], F32, name=f"a_ps{h}") for h in range(HALVES)]
+        for h in range(HALVES):
+            first_stage(
+                a_ps[h], w_sb, W_AT,
+                xt_picked[:, h * H : (h + 1) * H].bitcast(E4M3X4),
+                planes[:, XT_AT + h * H : XT_AT + (h + 1) * H],
+            )
+
+        q_sb = tile("q_sb", [P, (J + 1) * PACK], F32)
+        nc.vector.memset(q_sb[:, 0:PACK], 0.0)
+        HW = H * PACK
+        for h in range(HALVES):
+            nc.scalar.copy(
+                q_sb[:, PACK + h * HW : PACK + (h + 1) * HW].rearrange("p (j t) -> p j t", t=PACK),
+                q_ps[h][:].rearrange("p t j -> p j t"),
+            )
+        tz_picked = tile("tz_picked", [P, NT, J], F32)
+        for u in range(NT):
+            nc.scalar.activation(tz_picked[:, u, :], tz_sb[:, u, :].indirect(list_tz[:]), ACT.Copy)
+
+        step = [tile(f"step{h}", [P, HW], F32) for h in range(HALVES)]
+        hid_bf = [tile(f"hid_bf{h}", [P, HW], BF16) for h in range(HALVES)]
+        hid_codes = [tile(f"hid_codes{h}", [P, H], U32) for h in range(HALVES)]
+        hid_scales = [tile(f"hid_scales{h}", [P, H], U8) for h in range(HALVES)]
+        p_ps = [ps.tile([P, NT, H], F32, name=f"p_ps{h}") for h in range(HALVES)]
+        floored = [tile(f"floored{h}", [P, NT, H], F32) for h in range(HALVES)]
+        res = [tile(f"res{h}", [P, NT, H], F32) for h in range(HALVES)]
+        out_rows = out.rearrange("(u p) j -> p u j", p=P)
+
+        def take_step(h):
+            nc.vector.scalar_tensor_tensor(
+                step[h][:], q_sb[:, h * HW : (h + 1) * HW], STEP,
+                q_sb[:, PACK + h * HW : PACK + (h + 1) * HW], ALU.mult, ALU.add,
+            )
+
+        def take_larger(h):
+            nc.vector.tensor_tensor(
+                hid_bf[h][:].rearrange("p (j t) -> p j t", t=PACK),
+                step[h][:].rearrange("p (j t) -> p j t", t=PACK),
+                a_ps[h][:].rearrange("p t j -> p j t"),
+                ALU.max,
+            )
+
+        def second_stage(h):
+            nc.vector.quantize_mx(hid_codes[h][:].bitcast(E5M2X4), hid_scales[h][:], hid_bf[h][:])
+            for u in range(NT):
+                nc.tensor.matmul_mx(
+                    p_ps[h][:, u, :],
+                    lhsT=wb_sb[:, 2 * P * u : 2 * P * (u + 1)].bitcast(E2M1X4),
+                    lhsT_scale=planes[:, WB_AT + P * u : WB_AT + P * (u + 1)],
+                    rhs=hid_codes[h][:].bitcast(E5M2X4),
+                    rhs_scale=hid_scales[h][:],
+                    start=True,
+                    stop=True,
+                )
+
+        def floor(h):
+            nc.vector.tensor_tensor(floored[h][:], p_ps[h][:], tz_picked[:, :, h * H : (h + 1) * H], ALU.max)
+
+        def weigh(h):
+            rw_h = rw_ps[:, :, h * H // 2 : (h + 1) * H // 2].rearrange("p e n -> p n e")
+            nc.vector.tensor_tensor(
+                res[h][:].rearrange("p u (n e) -> p u n e", e=2),
+                floored[h][:].rearrange("p u (n e) -> p u n e", e=2),
+                rw_h.unsqueeze(1).to_broadcast([P, NT, H // 2, 2]),
+                ALU.mult,
+            )
+            nc.sync.dma_start(out_rows[:, :, h * H : (h + 1) * H], res[h][:])
+
+        take_step(0)
+        take_step(1)
+        take_larger(0)
+        take_larger(1)
+        second_stage(0)
+        second_stage(1)
+        floor(0)
+        floor(1)
+        weigh(0)
+        weigh(1)

@@ -37,8 +37,8 @@ def tile_list_two_picked_gated_stepgap_floored_kernel(
         sb = ctx.enter_context(tc.tile_pool(name="sb", bufs=1))
         ps = ctx.enter_context(tc.psum_pool(name="ps", bufs=1))
 
-        def tile(name, shape, dtype):
-            return sb.tile(shape, dtype, name=name, align_bytes=64)
+        def tile(name, shape, dtype, tag=None):
+            return sb.tile(shape, dtype, name=name, tag=tag or name, align_bytes=64)
 
         list_xt = tile("list_xt", [P, J // 16], U16)
         list_xo = tile("list_xo", [P, J // 16], U16)
@@ -47,11 +47,7 @@ def tile_list_two_picked_gated_stepgap_floored_kernel(
         xo_sb = [tile(f"xo_sb{t}", [P, Z], F32) for t in range(PACK)]
         fl_sb = tile("fl_sb", [P, PACK], F32)
         rw_sb = tile("rw_sb", [P, 2], F32)
-        tz_sb = tile("tz_sb", [P, NT, M], F32)
-        xt_raw = tile("xt_raw", [P, T], I32)
-        w_raw = tile("w_raw", [P, 2 * R], U8)
         w2_raw = tile("w2_raw", [P, 2 * R], U8)
-        wb_sb = tile("wb_sb", [P, 2 * N], U8)
         xs_raw = tile("xs_raw", [P, T], U8)
         ws_raw = tile("ws_raw", [P, 2 * R], U8)
         planes = tile("planes", [P, PLANE_COLS], U8)
@@ -61,24 +57,20 @@ def tile_list_two_picked_gated_stepgap_floored_kernel(
         nc.vector.memset(planes[:, WB_AT:XT_AT].bitcast(I32), 0)
 
         xo_rows = xo.rearrange("(p t) z -> p t z", t=PACK)
-        nc.sync.dma_start(list_xo[:], offs2)
         nc.sync.dma_start(so_sb[:], so.rearrange("(p t) j -> p t j", t=PACK))
-        nc.sync.dma_start(xo_sb[0][:], xo_rows[:, 0, :])
+        nc.sync.dma_start(list_xo[:], offs2)
+        nc.sync.dma_start(ws_raw[0:16, R : 2 * R].bitcast(I32), w2_scales[0].bitcast(I32))
+        nc.sync.dma_start(ws_raw[0:16, 0:R].bitcast(I32), w_scales[0].bitcast(I32))
+        nc.sync.dma_start(xs_raw[0:16, :].bitcast(I32), xt_scales[0].bitcast(I32))
         nc.sync.dma_start(list_xt[:], offs)
-        nc.scalar.dma_start(ws_raw[0:16, R : 2 * R].bitcast(I32), w2_scales[0].bitcast(I32))
-        nc.scalar.dma_start(ws_raw[0:16, 0:R].bitcast(I32), w_scales[0].bitcast(I32))
-        nc.scalar.dma_start(xs_raw[0:16, :].bitcast(I32), xt_scales[0].bitcast(I32))
-        nc.scalar.dma_start(planes[0:16, WB_AT:XT_AT].bitcast(I32), wb_scales[0].bitcast(I32))
+        nc.sync.dma_start(planes[0:16, WB_AT:XT_AT].bitcast(I32), wb_scales[0].bitcast(I32))
+        nc.sync.dma_start(xo_sb[0][:], xo_rows[:, 0, :])
         nc.sync.dma_start(w2_raw[:].bitcast(I32), w2_words[0].bitcast(I32))
         nc.sync.dma_start(list_tz[:], offs3)
         for t in range(1, PACK):
             nc.sync.dma_start(xo_sb[t][:], xo_rows[:, t, :])
-        nc.sync.dma_start(xt_raw[:], xt_words[0].rearrange("p c b -> p (c b)").bitcast(I32))
-        nc.sync.dma_start(w_raw[:].bitcast(I32), w_words[0].bitcast(I32))
-        nc.sync.dma_start(tz_sb[:], tz.rearrange("(u p) m -> p u m", p=P))
         nc.gpsimd.dma_start(fl_sb[:], fl.rearrange("(p t) o -> p (t o)", t=PACK))
         nc.gpsimd.dma_start(rw_sb[:], rw.rearrange("o (p e) -> p (o e)", e=2))
-        nc.gpsimd.dma_start(wb_sb[:].bitcast(I32), wb_words[0].bitcast(I32))
 
         ident = tile("ident", [P, P], F32)
         make_identity(nc, ident[:])
@@ -104,6 +96,15 @@ def tile_list_two_picked_gated_stepgap_floored_kernel(
                 planes[32 * quad : 32 * quad + 4, :].bitcast(I32),
                 planes[4 * quad : 4 * quad + 4, :].bitcast(I32),
             )
+
+        xt_raw = tile("xt_raw", [P, T], I32, tag="xs_raw")
+        w_raw = tile("w_raw", [P, 2 * R], U8, tag="ws_raw")
+        tz_sb = tile("tz_sb", [P, NT, M], F32, tag="sig")
+        nc.sync.dma_start(xt_raw[:], xt_words[0].rearrange("p c b -> p (c b)").bitcast(I32))
+        nc.sync.dma_start(w_raw[:].bitcast(I32), w_words[0].bitcast(I32))
+        nc.sync.dma_start(tz_sb[:], tz.rearrange("(u p) m -> p u m", p=P))
+        wb_sb = tile("wb_sb", [P, 2 * N], U8, tag="so_sb")
+        nc.sync.dma_start(wb_sb[:].bitcast(I32), wb_words[0].bitcast(I32))
 
         def deal_words(dst, src):
             nc.vector.tensor_copy(
@@ -134,66 +135,69 @@ def tile_list_two_picked_gated_stepgap_floored_kernel(
         for h in range(HALVES):
             nc.vector.quantize_mx(u2_codes[h][:].bitcast(E5M2X4), u2_scales[h][:], u2_bf[h][:])
 
-        def first_stage(bank, words, plane_at, rhs, rhs_scale):
-            for t in range(PACK):
-                nc.tensor.matmul_mx(
-                    bank[:, t, :],
-                    lhsT=words[:, 2 * P * t : 2 * P * (t + 1)].bitcast(E2M1X4),
-                    lhsT_scale=planes[:, plane_at + P * t : plane_at + P * (t + 1)],
-                    rhs=rhs,
-                    rhs_scale=rhs_scale,
-                    start=True,
-                    stop=True,
-                )
+        def first_stage(dst, t, words, plane_at, rhs, rhs_scale):
+            nc.tensor.matmul_mx(
+                dst,
+                lhsT=words[:, 2 * P * t : 2 * P * (t + 1)].bitcast(E2M1X4),
+                lhsT_scale=planes[:, plane_at + P * t : plane_at + P * (t + 1)],
+                rhs=rhs,
+                rhs_scale=rhs_scale,
+                start=True,
+                stop=True,
+            )
 
-        q_ps = [ps.tile([P, PACK, H], F32, name=f"q_ps{h}") for h in range(HALVES)]
+        q_ps = [[ps.tile([P, 2, H], F32, name=f"q_ps{h}{g}") for g in range(2)] for h in range(HALVES)]
         for h in range(HALVES):
-            first_stage(q_ps[h], w2_sb, W2_AT, u2_codes[h][:].bitcast(E5M2X4), u2_scales[h][:])
+            for t in range(PACK):
+                first_stage(q_ps[h][t // 2][:, t % 2, :], t, w2_sb, W2_AT, u2_codes[h][:].bitcast(E5M2X4), u2_scales[h][:])
 
-        xt_picked = tile("xt_picked", [P, J], U32)
+        xt_picked = tile("xt_picked", [P, J], U32, tag="u2_bf1")
         nc.vector.tensor_copy(xt_picked[:], xt_raw[:].bitcast(U32).indirect(list_xt[:]))
-        w_sb = tile("w_sb", [P, 2 * R], U8)
+        w_sb = tile("w_sb", [P, 2 * R], U8, tag="u2_bf0")
         deal_words(w_sb, w_raw)
         a_ps = [ps.tile([P, PACK, H], F32, name=f"a_ps{h}") for h in range(HALVES)]
         for h in range(HALVES):
-            first_stage(
-                a_ps[h], w_sb, W_AT,
-                xt_picked[:, h * H : (h + 1) * H].bitcast(E4M3X4),
-                planes[:, XT_AT + h * H : XT_AT + (h + 1) * H],
-            )
+            for t in range(PACK):
+                first_stage(
+                    a_ps[h][:, t, :], t, w_sb, W_AT,
+                    xt_picked[:, h * H : (h + 1) * H].bitcast(E4M3X4),
+                    planes[:, XT_AT + h * H : XT_AT + (h + 1) * H],
+                )
 
-        q_sb = tile("q_sb", [P, (J + 1) * PACK], F32)
-        nc.vector.memset(q_sb[:, 0:PACK], 0.0)
-        HW = H * PACK
+        q_sb = [tile(f"q_sb{g}", [P, (J + 1) * 2], F32) for g in range(2)]
+        for g in range(2):
+            nc.vector.memset(q_sb[g][:, 0:2], 0.0)
         for h in range(HALVES):
-            nc.scalar.copy(
-                q_sb[:, PACK + h * HW : PACK + (h + 1) * HW].rearrange("p (j t) -> p j t", t=PACK),
-                q_ps[h][:].rearrange("p t j -> p j t"),
-            )
-        tz_picked = tile("tz_picked", [P, NT, J], F32)
+            for g in range(2):
+                nc.scalar.copy(
+                    q_sb[g][:, 2 + 2 * h * H : 2 + 2 * (h + 1) * H].rearrange("p (j e) -> p j e", e=2),
+                    q_ps[h][g][:].rearrange("p e j -> p j e"),
+                )
+        tz_picked = tile("tz_picked", [P, NT, J], F32, tag="u2_codes1")
         for u in range(NT):
             nc.scalar.activation(tz_picked[:, u, :], tz_sb[:, u, :].indirect(list_tz[:]), ACT.Copy)
 
-        step = [tile(f"step{h}", [P, HW], F32) for h in range(HALVES)]
+        HW = H * PACK
+        step = [tile(f"step{h}", [P, 2, 2 * H], F32) for h in range(HALVES)]
         hid_bf = [tile(f"hid_bf{h}", [P, HW], BF16) for h in range(HALVES)]
         hid_codes = [tile(f"hid_codes{h}", [P, H], U32) for h in range(HALVES)]
         hid_scales = [tile(f"hid_scales{h}", [P, H], U8) for h in range(HALVES)]
-        p_ps = [ps.tile([P, NT, H], F32, name=f"p_ps{h}") for h in range(HALVES)]
+        p_ps = [[ps.tile([P, H], F32, name=f"p_ps{h}{u}", tag=f"q_ps{h}{u}") for u in range(NT)] for h in range(HALVES)]
         floored = [tile(f"floored{h}", [P, NT, H], F32) for h in range(HALVES)]
         res = [tile(f"res{h}", [P, NT, H], F32) for h in range(HALVES)]
         out_rows = out.rearrange("(u p) j -> p u j", p=P)
 
-        def take_step(h):
+        def take_step(h, g):
             nc.vector.scalar_tensor_tensor(
-                step[h][:], q_sb[:, h * HW : (h + 1) * HW], STEP,
-                q_sb[:, PACK + h * HW : PACK + (h + 1) * HW], ALU.mult, ALU.add,
+                step[h][:, g, :], q_sb[g][:, 2 * h * H : 2 * (h + 1) * H], STEP,
+                q_sb[g][:, 2 + 2 * h * H : 2 + 2 * (h + 1) * H], ALU.mult, ALU.add,
             )
 
         def take_larger(h):
             nc.vector.tensor_tensor(
-                hid_bf[h][:].rearrange("p (j t) -> p j t", t=PACK),
-                step[h][:].rearrange("p (j t) -> p j t", t=PACK),
-                a_ps[h][:].rearrange("p t j -> p j t"),
+                hid_bf[h][:].rearrange("p (j g e) -> p j g e", g=2, e=2),
+                step[h][:].rearrange("p g (j e) -> p j g e", e=2),
+                a_ps[h][:].rearrange("p (g e) j -> p j g e", e=2),
                 ALU.max,
             )
 
@@ -201,7 +205,7 @@ def tile_list_two_picked_gated_stepgap_floored_kernel(
             nc.vector.quantize_mx(hid_codes[h][:].bitcast(E5M2X4), hid_scales[h][:], hid_bf[h][:])
             for u in range(NT):
                 nc.tensor.matmul_mx(
-                    p_ps[h][:, u, :],
+                    p_ps[h][u][:],
                     lhsT=wb_sb[:, 2 * P * u : 2 * P * (u + 1)].bitcast(E2M1X4),
                     lhsT_scale=planes[:, WB_AT + P * u : WB_AT + P * (u + 1)],
                     rhs=hid_codes[h][:].bitcast(E5M2X4),
@@ -211,25 +215,29 @@ def tile_list_two_picked_gated_stepgap_floored_kernel(
                 )
 
         def floor(h):
-            nc.vector.tensor_tensor(floored[h][:], p_ps[h][:], tz_picked[:, :, h * H : (h + 1) * H], ALU.max)
+            for u in range(NT):
+                nc.vector.tensor_tensor(floored[h][:, u, :], p_ps[h][u][:], tz_picked[:, u, h * H : (h + 1) * H], ALU.max)
 
         def weigh(h):
             rw_h = rw_ps[:, :, h * H // 2 : (h + 1) * H // 2].rearrange("p e n -> p n e")
-            nc.vector.tensor_tensor(
-                res[h][:].rearrange("p u (n e) -> p u n e", e=2),
-                floored[h][:].rearrange("p u (n e) -> p u n e", e=2),
-                rw_h.unsqueeze(1).to_broadcast([P, NT, H // 2, 2]),
-                ALU.mult,
-            )
-            nc.sync.dma_start(out_rows[:, :, h * H : (h + 1) * H], res[h][:])
+            for u in range(NT):
+                nc.vector.tensor_tensor(
+                    res[h][:, u, :].rearrange("p (n e) -> p n e", e=2),
+                    floored[h][:, u, :].rearrange("p (n e) -> p n e", e=2),
+                    rw_h,
+                    ALU.mult,
+                )
+            (nc.sync, nc.scalar)[h].dma_start(out_rows[:, :, h * H : (h + 1) * H], res[h][:])
 
-        take_step(0)
-        take_step(1)
+        take_step(0, 0)
+        take_step(0, 1)
+        take_step(1, 0)
         take_larger(0)
-        take_larger(1)
+        take_step(1, 1)
         second_stage(0)
-        second_stage(1)
+        take_larger(1)
         floor(0)
-        floor(1)
+        second_stage(1)
         weigh(0)
+        floor(1)
         weigh(1)

from contextlib import ExitStack

import concourse.mybir as mybir
from concourse.masks import make_identity

K, T, J, R, F, Z, N, M = 512, 512, 256, 512, 512, 1024, 256, 512
FLOPS = 2 * J * (K * R + F * R + R * N)

F32 = mybir.dt.float32
BF16 = mybir.dt.bfloat16
I32 = mybir.dt.int32
U32 = mybir.dt.uint32
U16 = mybir.dt.uint16
U8 = mybir.dt.uint8
E4M3X4 = mybir.dt.float8_e4m3fn_x4
E5M2X4 = mybir.dt.float8_e5m2_x4
E2M1X4 = mybir.dt.float4_e2m1fn_x4
ALU = mybir.AluOpType
ACT = mybir.ActivationFunctionType

P = 128
PACK = 4
HALVES = 2
H = J // HALVES
NT = N // P
STEP = -0.6
W_AT, W2_AT, WB_AT, XT_AT = 0, R, 2 * R, 2 * R + N
PLANE_COLS = XT_AT + J


def tile_list_two_picked_gated_stepgap_floored_kernel(
    tc, xt_words, xt_scales, w_words, w_scales, xo, fl, so, w2_words, w2_scales,
    wb_words, wb_scales, tz, rw, offs, offs2, offs3, out,
):
    nc = tc.nc
    with ExitStack() as ctx:
        sb = ctx.enter_context(tc.tile_pool(name="sb", bufs=1))
        ps = ctx.enter_context(tc.psum_pool(name="ps", bufs=1))

        def tile(name, shape, dtype, tag=None):
            return sb.tile(shape, dtype, name=name, tag=tag or name, align_bytes=64)

        list_xt = tile("list_xt", [P, J // 16], U16)
        list_xo = tile("list_xo", [P, J // 16], U16)
        list_tz = tile("list_tz", [P, J // 16], U16)
        so_sb = tile("so_sb", [P, PACK, J], F32)
        xo_sb = [tile(f"xo_sb{t}", [P, Z], F32) for t in range(PACK)]
        fl_sb = tile("fl_sb", [P, PACK], F32)
        rw_sb = tile("rw_sb", [P, 2], F32)
        w2_raw = tile("w2_raw", [P, 2 * R], U8)
        xs_raw = tile("xs_raw", [P, T], U8)
        ws_raw = tile("ws_raw", [P, 2 * R], U8)
        planes = tile("planes", [P, PLANE_COLS], U8)

        nc.vector.memset(ws_raw[:].bitcast(I32), 0)
        nc.vector.memset(xs_raw[:].bitcast(I32), 0)
        nc.vector.memset(planes[:, WB_AT:XT_AT].bitcast(I32), 0)

        xo_rows = xo.rearrange("(p t) z -> p t z", t=PACK)
        nc.sync.dma_start(so_sb[:], so.rearrange("(p t) j -> p t j", t=PACK))
        nc.sync.dma_start(list_xo[:], offs2)
        nc.sync.dma_start(ws_raw[0:16, R : 2 * R].bitcast(I32), w2_scales[0].bitcast(I32))
        nc.sync.dma_start(ws_raw[0:16, 0:R].bitcast(I32), w_scales[0].bitcast(I32))
        nc.sync.dma_start(xs_raw[0:16, :].bitcast(I32), xt_scales[0].bitcast(I32))
        nc.sync.dma_start(list_xt[:], offs)
        nc.sync.dma_start(planes[0:16, WB_AT:XT_AT].bitcast(I32), wb_scales[0].bitcast(I32))
        nc.sync.dma_start(xo_sb[0][:], xo_rows[:, 0, :])
        nc.sync.dma_start(w2_raw[:].bitcast(I32), w2_words[0].bitcast(I32))
        nc.sync.dma_start(list_tz[:], offs3)
        for t in range(1, PACK):
            nc.sync.dma_start(xo_sb[t][:], xo_rows[:, t, :])
        nc.gpsimd.dma_start(fl_sb[:], fl.rearrange("(p t) o -> p (t o)", t=PACK))
        nc.gpsimd.dma_start(rw_sb[:], rw.rearrange("o (p e) -> p (o e)", e=2))

        ident = tile("ident", [P, P], F32)
        make_identity(nc, ident[:])
        rw_ps = ps.tile([P, 2, P], F32, name="rw_ps")
        for e in range(2):
            nc.tensor.transpose(rw_ps[:, e, :], rw_sb[:, e : e + 1].to_broadcast([P, P]), ident[:])

        sig = tile("sig", [P, PACK, J], F32)
        gate = tile("gate", [P, PACK, J], F32)
        for t in range(PACK):
            nc.scalar.activation(sig[:, t, :], so_sb[:, t, :], ACT.Sigmoid)
            nc.scalar.activation(gate[:, t, :], sig[:, t, :], ACT.Copy, scale=fl_sb[:, t : t + 1])

        nc.vector.tensor_copy(
            planes[:, W_AT:WB_AT].rearrange("p (s t m) -> p s t m", s=2, t=PACK),
            ws_raw[:].rearrange("p (s m t) -> p s t m", s=2, t=PACK),
        )
        xs_picked = tile("xs_picked", [P, J], U8)
        nc.vector.tensor_copy(xs_picked[:], xs_raw[:].indirect(list_xt[:]))
        nc.vector.tensor_copy(planes[:, XT_AT:].bitcast(I32), xs_picked[:].bitcast(I32))
        for quad in range(1, 4):
            nc.scalar.dma_start(
                planes[32 * quad : 32 * quad + 4, :].bitcast(I32),
                planes[4 * quad : 4 * quad + 4, :].bitcast(I32),
            )

        xt_raw = tile("xt_raw", [P, T], I32, tag="xs_raw")
        w_raw = tile("w_raw", [P, 2 * R], U8, tag="ws_raw")
        tz_sb = tile("tz_sb", [P, NT, M], F32, tag="sig")
        nc.sync.dma_start(xt_raw[:], xt_words[0].rearrange("p c b -> p (c b)").bitcast(I32))
        nc.sync.dma_start(w_raw[:].bitcast(I32), w_words[0].bitcast(I32))
        nc.sync.dma_start(tz_sb[:], tz.rearrange("(u p) m -> p u m", p=P))
        wb_sb = tile("wb_sb", [P, 2 * N], U8, tag="so_sb")
        nc.sync.dma_start(wb_sb[:].bitcast(I32), wb_words[0].bitcast(I32))

        def deal_words(dst, src):
            nc.vector.tensor_copy(
                dst[:].bitcast(U16).rearrange("p (t m) -> p t m", t=PACK),
                src[:].bitcast(U16).rearrange("p (m t) -> p t m", t=PACK),
            )

        w2_sb = tile("w2_sb", [P, 2 * R], U8)
        deal_words(w2_sb, w2_raw)

        u2 = tile("u2", [P, PACK, J], F32)
        for t in range(PACK - 1):
            nc.vector.tensor_tensor(u2[:, t, :], xo_sb[t][:].indirect(list_xo[:]), gate[:, t, :], ALU.mult)
        last = PACK - 1
        for h in range(HALVES):
            cols = slice(h * H, (h + 1) * H)
            entries = list_xo[:, h * H // 16 : (h + 1) * H // 16]
            nc.vector.tensor_tensor(u2[:, last, cols], xo_sb[last][:].indirect(entries), gate[:, last, cols], ALU.mult)

        u2_bf = [tile(f"u2_bf{h}", [P, H * PACK], BF16) for h in range(HALVES)]
        u2_codes = [tile(f"u2_codes{h}", [P, H], U32) for h in range(HALVES)]
        u2_scales = [tile(f"u2_scales{h}", [P, H], U8) for h in range(HALVES)]
        for h in range(HALVES):
            nc.vector.tensor_copy(
                u2_bf[h][:].rearrange("p (c i t) -> p c t i", i=4, t=PACK),
                u2[:, :, h * H : (h + 1) * H].rearrange("p t (c i) -> p c t i", i=4),
            )
        for h in range(HALVES):
            nc.vector.quantize_mx(u2_codes[h][:].bitcast(E5M2X4), u2_scales[h][:], u2_bf[h][:])

        def first_stage(dst, t, words, plane_at, rhs, rhs_scale):
            nc.tensor.matmul_mx(
                dst,
                lhsT=words[:, 2 * P * t : 2 * P * (t + 1)].bitcast(E2M1X4),
                lhsT_scale=planes[:, plane_at + P * t : plane_at + P * (t + 1)],
                rhs=rhs,
                rhs_scale=rhs_scale,
                start=True,
                stop=True,
            )

        q_ps = [[ps.tile([P, 2, H], F32, name=f"q_ps{h}{g}") for g in range(2)] for h in range(HALVES)]
        for h in range(HALVES):
            for t in range(PACK):
                first_stage(q_ps[h][t // 2][:, t % 2, :], t, w2_sb, W2_AT, u2_codes[h][:].bitcast(E5M2X4), u2_scales[h][:])

        xt_picked = tile("xt_picked", [P, J], U32, tag="u2_bf1")
        nc.vector.tensor_copy(xt_picked[:], xt_raw[:].bitcast(U32).indirect(list_xt[:]))
        w_sb = tile("w_sb", [P, 2 * R], U8, tag="u2_bf0")
        deal_words(w_sb, w_raw)
        a_ps = [ps.tile([P, PACK, H], F32, name=f"a_ps{h}") for h in range(HALVES)]
        for h in range(HALVES):
            for t in range(PACK):
                first_stage(
                    a_ps[h][:, t, :], t, w_sb, W_AT,
                    xt_picked[:, h * H : (h + 1) * H].bitcast(E4M3X4),
                    planes[:, XT_AT + h * H : XT_AT + (h + 1) * H],
                )

        q_sb = [tile(f"q_sb{g}", [P, (J + 1) * 2], F32) for g in range(2)]
        for g in range(2):
            nc.vector.memset(q_sb[g][:, 0:2], 0.0)
        for h in range(HALVES):
            for g in range(2):
                nc.scalar.copy(
                    q_sb[g][:, 2 + 2 * h * H : 2 + 2 * (h + 1) * H].rearrange("p (j e) -> p j e", e=2),
                    q_ps[h][g][:].rearrange("p e j -> p j e"),
                )
        tz_picked = tile("tz_picked", [P, NT, J], F32, tag="u2_codes1")
        for u in range(NT):
            nc.scalar.activation(tz_picked[:, u, :], tz_sb[:, u, :].indirect(list_tz[:]), ACT.Copy)

        HW = H * PACK
        step = [tile(f"step{h}", [P, 2, 2 * H], F32) for h in range(HALVES)]
        hid_bf = [tile(f"hid_bf{h}", [P, HW], BF16) for h in range(HALVES)]
        hid_codes = [tile(f"hid_codes{h}", [P, H], U32) for h in range(HALVES)]
        hid_scales = [tile(f"hid_scales{h}", [P, H], U8) for h in range(HALVES)]
        p_ps = [[ps.tile([P, H], F32, name=f"p_ps{h}{u}", tag=f"q_ps{h}{u}") for u in range(NT)] for h in range(HALVES)]
        floored = [tile(f"floored{h}", [P, NT, H], F32) for h in range(HALVES)]
        res = [tile(f"res{h}", [P, NT, H], F32) for h in range(HALVES)]
        out_rows = out.rearrange("(u p) j -> p u j", p=P)

        def take_step(h, g):
            nc.vector.scalar_tensor_tensor(
                step[h][:, g, :], q_sb[g][:, 2 * h * H : 2 * (h + 1) * H], STEP,
                q_sb[g][:, 2 + 2 * h * H : 2 + 2 * (h + 1) * H], ALU.mult, ALU.add,
            )

        def take_larger(h):
            nc.vector.tensor_tensor(
                hid_bf[h][:].rearrange("p (j g e) -> p j g e", g=2, e=2),
                step[h][:].rearrange("p g (j e) -> p j g e", e=2),
                a_ps[h][:].rearrange("p (g e) j -> p j g e", e=2),
                ALU.max,
            )

        def second_stage(h):
            nc.vector.quantize_mx(hid_codes[h][:].bitcast(E5M2X4), hid_scales[h][:], hid_bf[h][:])
            for u in range(NT):
                nc.tensor.matmul_mx(
                    p_ps[h][u][:],
                    lhsT=wb_sb[:, 2 * P * u : 2 * P * (u + 1)].bitcast(E2M1X4),
                    lhsT_scale=planes[:, WB_AT + P * u : WB_AT + P * (u + 1)],
                    rhs=hid_codes[h][:].bitcast(E5M2X4),
                    rhs_scale=hid_scales[h][:],
                    start=True,
                    stop=True,
                )

        def floor(h):
            for u in range(NT):
                nc.vector.tensor_tensor(floored[h][:, u, :], p_ps[h][u][:], tz_picked[:, u, h * H : (h + 1) * H], ALU.max)

        def weigh(h):
            rw_h = rw_ps[:, :, h * H // 2 : (h + 1) * H // 2].rearrange("p e n -> p n e")
            for u in range(NT):
                nc.vector.tensor_tensor(
                    res[h][:, u, :].rearrange("p (n e) -> p n e", e=2),
                    floored[h][:, u, :].rearrange("p (n e) -> p n e", e=2),
                    rw_h,
                    ALU.mult,
                )
            (nc.sync, nc.scalar)[h].dma_start(out_rows[:, :, h * H : (h + 1) * H], res[h][:])

        take_step(0, 0)
        take_step(0, 1)
        take_step(1, 0)
        take_larger(0)
        take_step(1, 1)
        second_stage(0)
        take_larger(1)
        floor(0)
        second_stage(1)
        weigh(0)
        floor(1)
        weigh(1)
